import numpy as np
import ml_dtypes


def mxq(x, axis, fmt="e4m3"):
    dtype, down = {"e4m3": (ml_dtypes.float8_e4m3fn, 7), "e5m2": (ml_dtypes.float8_e5m2, 14)}[fmt]
    v = np.moveaxis(np.asarray(x, np.float32).astype(ml_dtypes.bfloat16).astype(np.float64), axis, -1)
    blocks = v.reshape(v.shape[:-1] + (-1, 32))
    amax = np.abs(blocks).max(-1, keepdims=True)
    byte = np.maximum(np.where(amax > 0, np.frexp(amax)[1] - 1 + 127, 0) - down, 1)
    scale = np.exp2(byte - 127.0)
    codes = (blocks / scale).astype(np.float32).astype(dtype).astype(np.float64)
    return np.moveaxis((codes * scale).reshape(v.shape), -1, axis)


WIDE = False


def mx_kscale(k):
    if not WIDE:
        return np.ones(k)
    levels = np.array([10, -10, 5, -5, 0])
    if k % 512:
        return np.exp2(np.random.permutation(np.resize(levels, k // 32))).repeat(32)
    a = np.empty((k // 512, 16))
    for p in range(k // 512):
        a[p, :8] = np.random.permutation(np.resize(levels, 8))
        for g in range(8):
            far = levels[np.abs(levels - a[p, g]) >= 10]
            a[p, g + 8] = far[np.random.randint(len(far))]
    return np.exp2(a.ravel()).repeat(32)


def f64(x):
    return np.asarray(x).astype(np.float64)


def striped(idx):
    return np.tile(idx.reshape(-1, 16).T, (8, 1)).astype(np.uint16)


def unstriped(offs):
    return offs[:16].T.reshape(-1).astype(np.int64)


def pack_weight(w):
    k, n = w.shape
    w = f64(np.asarray(w, np.float32).astype(ml_dtypes.bfloat16)).reshape(k // 32, 32, n)
    amax = np.abs(w).max(1)
    byte = np.clip(np.where(amax > 0, np.frexp(amax)[1] - 1 + 127 - 7, 1), 1, 254)
    scaled = (w * np.exp2(127.0 - byte)[:, None, :]).reshape(k, n).astype(np.float32)
    words = np.ascontiguousarray(scaled.reshape(k // 512, 128, 4, n).transpose(0, 1, 3, 2)).astype(ml_dtypes.float8_e4m3fn).view(np.uint8)
    return words, np.ascontiguousarray(byte.astype(np.uint8).reshape(k // 512, 16, n))


def unpack_weight(words, scales):
    g, p, n, _ = words.shape
    vals = np.ascontiguousarray(words).view(ml_dtypes.float8_e4m3fn).astype(np.float64) * np.repeat(np.exp2(scales.astype(np.float64) - 127.0), 8, axis=1)[..., None]
    return vals.transpose(0, 1, 3, 2).reshape(g * 512, n)


def sigmoid(v):
    return 1.0 / (1.0 + np.exp(-np.maximum(v, -700.0)))


K, T, S, H, V, Z, W = 512, 1024, 512, 512, 256, 512, 2048
P = 2 ** 7


def setup_inputs():
    n = np.random.standard_normal
    s = mx_kscale(K)[:, None]
    packed_xT = pack_weight(n((K, T)) * s)
    packed_eT = pack_weight(n((K, W)) * s)
    return {
        "x_words": packed_xT[0],
        "x_scales": packed_xT[1],
        "w1": (n((K, H)) / np.sqrt(K) / s).astype(np.float32),
        "w2": (n((K, H)) / np.sqrt(K) / s).astype(np.float32),
        "lam": (np.random.uniform(0.2, 0.8, (H, V))).astype(np.float32),
        "e_words": packed_eT[0],
        "e_scales": packed_eT[1],
        "unit": (np.random.uniform(0.6, 1.4, (K, 1)) / np.sqrt(K) / s).astype(np.float32),
        "tmp": (np.tile(np.random.uniform(0.6, 1.5, W), (P, 1))).astype(np.float32),
        "offs": striped(np.random.permutation(T)[:S]),
        "cra": striped(np.random.permutation(S)[:V]),
        "crb": striped(np.random.permutation(S)[:V]),
        "prt": striped(np.random.permutation(W)[:Z]),
    }


def reference(x_words, x_scales, w1, w2, lam, e_words, e_scales, unit, tmp, offs, cra, crb, prt):
    xq = unpack_weight(x_words, x_scales)[:, unstriped(offs)]
    y = mxq(f64(w1), 0, "e4m3").T @ xq
    a_ = y[:, unstriped(cra)]
    yv = mxq(f64(w2), 0, "e4m3").T @ xq
    b_ = yv[:, unstriped(crb)]
    lowr = np.minimum(a_, b_)
    mixv = f64(lam) * a_ + (-1.0 * f64(lam) + 1.0) * b_ - (0.4 * lowr)
    hid = f64(unit) * mixv
    e_prt = unpack_weight(e_words, e_scales)[:, unstriped(prt)]
    sc = mxq(hid, 0, "e4m3").T @ e_prt
    lt = sc * (f64(tmp)[:1][:, unstriped(prt)])
    mu = lt.mean(axis=1, keepdims=True)
    dl = lt - mu
    return sigmoid(dl) * lt

@@ -1,0 +1,188 @@
+from contextlib import ExitStack
+
+import concourse.mybir as mybir
+
+K, T, S, H, V, Z, W = 512, 1024, 512, 512, 256, 512, 2048
+FLOPS = 2 * K * H * S * 2 + 2 * H * V * Z
+
+F32 = mybir.dt.float32
+BF16 = mybir.dt.bfloat16
+I32 = mybir.dt.int32
+U32 = mybir.dt.uint32
+U16 = mybir.dt.uint16
+U8 = mybir.dt.uint8
+FP8X4 = mybir.dt.float8_e4m3fn_x4
+ALU = mybir.AluOpType
+ACT = mybir.ActivationFunctionType
+
+P = 128
+PACK = 4
+HALF_M = P // 2
+
+
+def tile_picked_ycroplb_sig_p_kernel(
+    tc, x_words, x_scales, w1, w2, lam, e_words, e_scales, unit, tmp, offs, cra, crb, prt, out
+):
+    nc = tc.nc
+    with ExitStack() as ctx:
+        keep = ctx.enter_context(tc.tile_pool(name="keep", bufs=1))
+        psum = ctx.enter_context(tc.psum_pool(name="psum", bufs=1))
+
+        def load_list(name, src):
+            lst = keep.tile(list(src.shape), U16, name=name)
+            nc.sync.dma_start(lst[:], src)
+            return lst
+
+        def load_words(name, src, width):
+            table = keep.tile([P, width], U32, name=name)
+            nc.sync.dma_start(table[:].bitcast(I32), src[0].rearrange("p n t -> p (n t)").bitcast(I32))
+            return table
+
+        def load_scales(name, src, width, clear, queue):
+            table = keep.tile([P, width], U8, name=name)
+            clear.memset(table[:].bitcast(I32), 0)
+            for q in range(4):
+                queue.dma_start(table[32 * q : 32 * q + 4, :].bitcast(I32), src[0, 4 * q : 4 * q + 4, :].bitcast(I32))
+            return table
+
+        def load_weight_half(name, w, h):
+            raw = keep.tile([P, PACK, H // 2], F32, name=name)
+            nc.sync.dma_start(raw[:], w.rearrange("(p j) c -> p j c", j=PACK)[:, :, h * (H // 2) : (h + 1) * (H // 2)])
+            return raw
+
+        xs_table = load_scales("xs_table", x_scales, T, nc.vector, nc.scalar)
+        es_table = load_scales("es_table", e_scales, W, nc.gpsimd, nc.scalar)
+        offs_t = load_list("offs_t", offs)
+        prt_t = load_list("prt_t", prt)
+        xw_table = load_words("xw_table", x_words, T)
+        w2_raw = [load_weight_half(f"w2_raw{h}", w2, h) for h in range(2)]
+        w1_raw = [load_weight_half(f"w1_raw{h}", w1, h) for h in range(2)]
+        unit_t = keep.tile([P, PACK], F32, name="unit_t")
+        nc.sync.dma_start(unit_t[:], unit.rearrange("(p t) o -> p (t o)", t=PACK))
+        crb_t = load_list("crb_t", crb)
+        cra_t = load_list("cra_t", cra)
+        lam_t = keep.tile([P, PACK, V], F32, name="lam_t")
+        nc.sync.dma_start(lam_t[:], lam.rearrange("(p t) v -> p t v", t=PACK))
+        ew_table = load_words("ew_table", e_words, W)
+        tmp_table = keep.tile([P, W], F32, name="tmp_table")
+        nc.sync.dma_start(tmp_table[:], tmp)
+
+        gain = keep.tile([P, PACK], F32, name="gain")
+        negative = keep.tile([P, PACK], F32, name="negative")
+        lam_gain = keep.tile([P, PACK], F32, name="lam_gain")
+        slope_gain = keep.tile([P, PACK], F32, name="slope_gain")
+        nc.gpsimd.tensor_scalar(gain[:], unit_t[:], 0.6, 0.0, ALU.mult, ALU.add)
+        nc.gpsimd.tensor_scalar(negative[:], unit_t[:], 0.0, None, ALU.is_lt)
+        nc.gpsimd.tensor_scalar(lam_gain[:], negative[:], -5.0, 2.5, ALU.mult, ALU.add)
+        nc.gpsimd.tensor_scalar(slope_gain[:], negative[:], 4.0 / 3.0, -2.0 / 3.0, ALU.mult, ALU.add)
+
+        def gather_packed(name, table, lst, n, dtype):
+            picked = keep.tile([P, n], dtype, name=name, align_bytes=64)
+            nc.vector.tensor_copy(picked[:], table[:].indirect(lst[:]))
+            return picked
+
+        xs = gather_packed("xs", xs_table, offs_t, S, U8)
+        xw = gather_packed("xw", xw_table, offs_t, S, U32)
+        es = gather_packed("es", es_table, prt_t, Z, U8)
+
+        def project(name, raws, first_bank):
+            codes = keep.tile([P, PACK, P], U32, name=f"{name}_codes", align_bytes=64)
+            scales = keep.tile([P, PACK, P], U8, name=f"{name}_scales", align_bytes=64)
+            grouped = []
+            for h in range(2):
+                g = keep.tile([P, PACK, HALF_M, PACK], BF16, name=f"{name}_grouped{h}", align_bytes=64)
+                dst = g[:].rearrange("p t m j -> p m j t")
+                src = raws[h][:].rearrange("p j (m t) -> p m j t", t=PACK)
+                if h == 0:
+                    nc.scalar.activation(dst, src, ACT.Copy)
+                else:
+                    nc.vector.tensor_copy(dst, src)
+                grouped.append(g)
+            for h in range(2):
+                for t in range(PACK):
+                    cols = slice(h * HALF_M, (h + 1) * HALF_M)
+                    nc.vector.quantize_mx(
+                        out=codes[:, t, cols].bitcast(FP8X4),
+                        scales=scales[:, t, cols],
+                        in_=grouped[h][:, t].rearrange("p m j -> p (m j)"),
+                    )
+            rows = []
+            for t in range(PACK):
+                bank = psum.tile([P, S], F32, name=f"bank{first_bank + t}")
+                nc.tensor.matmul_mx(
+                    out=bank[:],
+                    lhsT=codes[:, t].bitcast(FP8X4),
+                    lhsT_scale=scales[:, t],
+                    rhs=xw[:].bitcast(FP8X4),
+                    rhs_scale=xs[:],
+                    start=True,
+                    stop=True,
+                )
+                row = keep.tile([P, S], F32, name=f"{name}_row{t}")
+                nc.scalar.activation(row[:], bank[:], ACT.Copy, scale=gain[:, t : t + 1])
+                rows.append(row)
+            return rows
+
+        yv_rows = project("w2", w2_raw, 0)
+        b = keep.tile([P, PACK, V], F32, name="b")
+        for t in range(PACK):
+            if t < 2:
+                nc.vector.tensor_copy(b[:, t], yv_rows[t][:].indirect(crb_t[:]))
+            else:
+                nc.scalar.activation(b[:, t], yv_rows[t][:].indirect(crb_t[:]), ACT.Copy)
+        y_rows = project("w1", w1_raw, PACK)
+
+        share = keep.tile([P, PACK, V], F32, name="share")
+        for t in range(PACK):
+            nc.scalar.activation(share[:, t], lam_t[:, t], ACT.Identity, scale=lam_gain[:, t : t + 1], bias=negative[:, t : t + 1])
+
+        ew = gather_packed("ew", ew_table, prt_t, Z, U32)
+
+        d = keep.tile([P, PACK, V], F32, name="d")
+        slope = keep.tile([P, PACK, V], F32, name="slope")
+        pull = keep.tile([P, PACK, V], F32, name="pull")
+        for t in range(PACK):
+            nc.vector.tensor_tensor(d[:, t], y_rows[t][:].indirect(cra_t[:]), b[:, t], ALU.subtract)
+        for t in range(PACK):
+            nc.vector.scalar_tensor_tensor(slope[:, t], d[:, t], 0.0, share[:, t], ALU.is_lt, ALU.subtract)
+        for t in range(PACK):
+            nc.vector.scalar_tensor_tensor(pull[:, t], slope[:, t], slope_gain[:, t : t + 1], d[:, t], ALU.mult, ALU.mult)
+
+        temp = keep.tile([P, Z], F32, name="temp")
+        nc.scalar.activation(temp[:], tmp_table[:].indirect(prt_t[:]), ACT.Copy)
+
+        banks = []
+        for h in range(V // P):
+            vs = slice(h * P, (h + 1) * P)
+            hid = keep.tile([P, P, PACK], BF16, name=f"hid{h}", align_bytes=64)
+            nc.vector.tensor_tensor(
+                hid[:].rearrange("p (c i) t -> p c t i", i=4),
+                pull[:, :, vs].rearrange("p t (c i) -> p c t i", i=4),
+                b[:, :, vs].rearrange("p t (c i) -> p c t i", i=4),
+                ALU.add,
+            )
+            hid_codes = keep.tile([P, P], U32, name=f"hid_codes{h}", align_bytes=64)
+            hid_scales = keep.tile([P, P], U8, name=f"hid_scales{h}", align_bytes=64)
+            nc.vector.quantize_mx(
+                out=hid_codes[:].bitcast(FP8X4), scales=hid_scales[:], in_=hid[:].rearrange("p v t -> p (v t)")
+            )
+            bank = psum.tile([P, Z], F32, name=f"bank{h}")
+            nc.tensor.matmul_mx(
+                out=bank[:],
+                lhsT=hid_codes[:].bitcast(FP8X4),
+                lhsT_scale=hid_scales[:],
+                rhs=ew[:].bitcast(FP8X4),
+                rhs_scale=es[:],
+                start=True,
+                stop=True,
+            )
+            banks.append(bank)
+        for h in range(V // P):
+            lt = keep.tile([P, Z], F32, name=f"lt{h}")
+            neg_mean = keep.tile([P, 1], F32, name=f"neg_mean{h}")
+            nc.vector.scalar_tensor_tensor(lt[:], banks[h][:], -1.0 / Z, temp[:], ALU.mult, ALU.mult, accum_out=neg_mean[:])
+            gate = keep.tile([P, Z], F32, name=f"gate{h}")
+            nc.scalar.activation(gate[:], lt[:], ACT.Sigmoid, scale=-float(Z), bias=neg_mean[:])
+            result = keep.tile([P, Z], F32, name=f"result{h}")
+            nc.vector.scalar_tensor_tensor(result[:], lt[:], -float(Z), gate[:], ALU.mult, ALU.mult)
+            nc.sync.dma_start(out[h * P : (h + 1) * P, :], result[:])

@@ -46,24 +46,26 @@ def tile_picked_ycroplb_sig_p_kernel(
             return table
 
         def load_weight_half(name, w, h):
-            raw = keep.tile([P, PACK, H // 2], F32, name=name)
+            raw = keep.tile([P, PACK, H // 2], F32, name=name, align_bytes=64)
             nc.sync.dma_start(raw[:], w.rearrange("(p j) c -> p j c", j=PACK)[:, :, h * (H // 2) : (h + 1) * (H // 2)])
             return raw
 
-        xs_table = load_scales("xs_table", x_scales, T, nc.vector, nc.scalar)
-        es_table = load_scales("es_table", e_scales, W, nc.gpsimd, nc.scalar)
+        xs_table = load_scales("xs_table", x_scales, T, nc.gpsimd, nc.scalar)
         offs_t = load_list("offs_t", offs)
-        prt_t = load_list("prt_t", prt)
         xw_table = load_words("xw_table", x_words, T)
-        w2_raw = [load_weight_half(f"w2_raw{h}", w2, h) for h in range(2)]
-        w1_raw = [load_weight_half(f"w1_raw{h}", w1, h) for h in range(2)]
-        unit_t = keep.tile([P, PACK], F32, name="unit_t")
-        nc.sync.dma_start(unit_t[:], unit.rearrange("(p t) o -> p (t o)", t=PACK))
+        w2_whole = keep.tile([P, PACK, H], F32, name="w2_whole")
+        nc.sync.dma_start(w2_whole[:], w2.rearrange("(p j) c -> p j c", j=PACK))
+        w2_raw = [w2_whole[:, :, : PACK * 46], w2_whole[:, :, PACK * 46 :]]
         crb_t = load_list("crb_t", crb)
+        unit_t = keep.tile([P, PACK], F32, name="unit_t")
+        nc.gpsimd.dma_start(unit_t[:], unit.rearrange("(p t) o -> p (t o)", t=PACK))
+        w1_raw = [load_weight_half(f"w1_raw{h}", w1, h)[:] for h in range(2)]
+        prt_t = load_list("prt_t", prt)
+        es_table = load_scales("es_table", e_scales, W, nc.gpsimd, nc.sync)
+        ew_table = load_words("ew_table", e_words, W)
         cra_t = load_list("cra_t", cra)
         lam_t = keep.tile([P, PACK, V], F32, name="lam_t")
         nc.sync.dma_start(lam_t[:], lam.rearrange("(p t) v -> p t v", t=PACK))
-        ew_table = load_words("ew_table", e_words, W)
         tmp_table = keep.tile([P, W], F32, name="tmp_table")
         nc.sync.dma_start(tmp_table[:], tmp)
 
@@ -76,37 +78,29 @@ def tile_picked_ycroplb_sig_p_kernel(
         nc.gpsimd.tensor_scalar(lam_gain[:], negative[:], -5.0, 2.5, ALU.mult, ALU.add)
         nc.gpsimd.tensor_scalar(slope_gain[:], negative[:], 4.0 / 3.0, -2.0 / 3.0, ALU.mult, ALU.add)
 
-        def gather_packed(name, table, lst, n, dtype):
-            picked = keep.tile([P, n], dtype, name=name, align_bytes=64)
+        def gather_packed(name, table, lst, n, dtype, tag):
+            picked = keep.tile([P, n], dtype, name=name, tag=tag, align_bytes=64)
             nc.vector.tensor_copy(picked[:], table[:].indirect(lst[:]))
             return picked
 
-        xs = gather_packed("xs", xs_table, offs_t, S, U8)
-        xw = gather_packed("xw", xw_table, offs_t, S, U32)
-        es = gather_packed("es", es_table, prt_t, Z, U8)
+        xs = gather_packed("xs", xs_table, offs_t, S, U8, "xs")
+        xw = gather_packed("xw", xw_table, offs_t, S, U32, "xw")
 
-        def project(name, raws, first_bank):
+        def deal(engine, dst, src):
+            dst = dst.rearrange("p t m j -> p m j t")
+            src = src.rearrange("p j (m t) -> p m j t", t=PACK)
+            if engine is nc.scalar:
+                nc.scalar.activation(dst, src, ACT.Copy)
+            else:
+                nc.vector.tensor_copy(dst, src)
+
+        def weight_tiles(name):
             codes = keep.tile([P, PACK, P], U32, name=f"{name}_codes", align_bytes=64)
             scales = keep.tile([P, PACK, P], U8, name=f"{name}_scales", align_bytes=64)
-            grouped = []
-            for h in range(2):
-                g = keep.tile([P, PACK, HALF_M, PACK], BF16, name=f"{name}_grouped{h}", align_bytes=64)
-                dst = g[:].rearrange("p t m j -> p m j t")
-                src = raws[h][:].rearrange("p j (m t) -> p m j t", t=PACK)
-                if h == 0:
-                    nc.scalar.activation(dst, src, ACT.Copy)
-                else:
-                    nc.vector.tensor_copy(dst, src)
-                grouped.append(g)
-            for h in range(2):
-                for t in range(PACK):
-                    cols = slice(h * HALF_M, (h + 1) * HALF_M)
-                    nc.vector.quantize_mx(
-                        out=codes[:, t, cols].bitcast(FP8X4),
-                        scales=scales[:, t, cols],
-                        in_=grouped[h][:, t].rearrange("p m j -> p (m j)"),
-                    )
-            rows = []
+            return codes, scales
+
+        def project(codes, scales, first_bank):
+            banks = []
             for t in range(PACK):
                 bank = psum.tile([P, S], F32, name=f"bank{first_bank + t}")
                 nc.tensor.matmul_mx(
@@ -118,37 +112,63 @@ def tile_picked_ycroplb_sig_p_kernel(
                     start=True,
                     stop=True,
                 )
-                row = keep.tile([P, S], F32, name=f"{name}_row{t}")
-                nc.scalar.activation(row[:], bank[:], ACT.Copy, scale=gain[:, t : t + 1])
-                rows.append(row)
-            return rows
+                banks.append(bank)
+            return banks
 
-        yv_rows = project("w2", w2_raw, 0)
+        def evict(name, bank, t):
+            row = keep.tile([P, S], F32, name=f"{name}_row{t}")
+            nc.scalar.activation(row[:], bank[:], ACT.Copy, scale=gain[:, t : t + 1])
+            return row
+
+        w2_codes, w2_scales = weight_tiles("w2")
+        w2_dealt = keep.tile([P, PACK, P, PACK], BF16, name="w2_dealt", tag="dealt", align_bytes=64)
+        deal(nc.scalar, w2_dealt[:, :, :46], w2_raw[0])
+        deal(nc.vector, w2_dealt[:, :, 46:], w2_raw[1])
+        for ts in (slice(0, 2), slice(2, 4)):
+            nc.vector.quantize_mx(
+                out=w2_codes[:, ts].rearrange("p t m -> p (t m)").bitcast(FP8X4),
+                scales=w2_scales[:, ts].rearrange("p t m -> p (t m)"),
+                in_=w2_dealt[:, ts].rearrange("p t m j -> p (t m j)"),
+            )
+        yv_banks = project(w2_codes, w2_scales, 0)
+
+        w1_codes, w1_scales = weight_tiles("w1")
+        w1_dealt = [
+            keep.tile([P, PACK, HALF_M, PACK], BF16, name="w1_dealt0", align_bytes=64),
+            keep.tile([P, PACK, HALF_M, PACK], BF16, name="w1_dealt1", tag="dealt", align_bytes=64),
+        ]
+        deal(nc.scalar, w1_dealt[0][:], w1_raw[0])
+        deal(nc.vector, w1_dealt[1][:], w1_raw[1])
+        yv_rows = [evict("w2", yv_banks[t], t) for t in range(PACK)]
+        for h in range(2):
+            for t in range(PACK):
+                cols = slice(h * HALF_M, (h + 1) * HALF_M)
+                nc.vector.quantize_mx(
+                    out=w1_codes[:, t, cols].bitcast(FP8X4),
+                    scales=w1_scales[:, t, cols],
+                    in_=w1_dealt[h][:, t].rearrange("p m j -> p (m j)"),
+                )
+        y_banks = project(w1_codes, w1_scales, PACK)
+        es = gather_packed("es", es_table, prt_t, Z, U8, "w1_dealt0")
+        ew = gather_packed("ew", ew_table, prt_t, Z, U32, "dealt")
+
         b = keep.tile([P, PACK, V], F32, name="b")
-        for t in range(PACK):
-            if t < 2:
-                nc.vector.tensor_copy(b[:, t], yv_rows[t][:].indirect(crb_t[:]))
-            else:
-                nc.scalar.activation(b[:, t], yv_rows[t][:].indirect(crb_t[:]), ACT.Copy)
-        y_rows = project("w1", w1_raw, PACK)
-
-        share = keep.tile([P, PACK, V], F32, name="share")
-        for t in range(PACK):
-            nc.scalar.activation(share[:, t], lam_t[:, t], ACT.Identity, scale=lam_gain[:, t : t + 1], bias=negative[:, t : t + 1])
-
-        ew = gather_packed("ew", ew_table, prt_t, Z, U32)
-
         d = keep.tile([P, PACK, V], F32, name="d")
         slope = keep.tile([P, PACK, V], F32, name="slope")
         pull = keep.tile([P, PACK, V], F32, name="pull")
+        share = keep.tile([P, PACK, V], F32, name="share")
         for t in range(PACK):
-            nc.vector.tensor_tensor(d[:, t], y_rows[t][:].indirect(cra_t[:]), b[:, t], ALU.subtract)
+            nc.gpsimd.tensor_scalar(share[:, t], lam_t[:, t], lam_gain[:, t : t + 1], negative[:, t : t + 1], ALU.mult, ALU.add)
         for t in range(PACK):
-            nc.vector.scalar_tensor_tensor(slope[:, t], d[:, t], 0.0, share[:, t], ALU.is_lt, ALU.subtract)
-        for t in range(PACK):
-            nc.vector.scalar_tensor_tensor(pull[:, t], slope[:, t], slope_gain[:, t : t + 1], d[:, t], ALU.mult, ALU.mult)
+            nc.scalar.activation(b[:, t], yv_rows[t][:].indirect(crb_t[:]), ACT.Copy)
+            y_row = evict("w1", y_banks[t], t)
+            nc.vector.tensor_tensor(d[:, t], y_row[:].indirect(cra_t[:]), b[:, t], ALU.subtract)
+        for ts in (slice(0, 2), slice(2, 4)):
+            nc.vector.scalar_tensor_tensor(slope[:, ts], d[:, ts], 0.0, share[:, ts], ALU.is_lt, ALU.subtract)
+            for t in range(ts.start, ts.stop):
+                nc.vector.scalar_tensor_tensor(pull[:, t], slope[:, t], slope_gain[:, t : t + 1], d[:, t], ALU.mult, ALU.mult)
 
-        temp = keep.tile([P, Z], F32, name="temp")
+        temp = keep.tile([P, Z], F32, name="temp", tag="w1_row3")
         nc.scalar.activation(temp[:], tmp_table[:].indirect(prt_t[:]), ACT.Copy)
 
         banks = []

from contextlib import ExitStack

import concourse.mybir as mybir

K, T, S, H, V, Z, W = 512, 1024, 512, 512, 256, 512, 2048
FLOPS = 2 * K * H * S * 2 + 2 * H * V * Z

F32 = mybir.dt.float32
BF16 = mybir.dt.bfloat16
I32 = mybir.dt.int32
U32 = mybir.dt.uint32
U16 = mybir.dt.uint16
U8 = mybir.dt.uint8
FP8X4 = mybir.dt.float8_e4m3fn_x4
ALU = mybir.AluOpType
ACT = mybir.ActivationFunctionType

P = 128
PACK = 4
HALF_M = P // 2


def tile_picked_ycroplb_sig_p_kernel(
    tc, x_words, x_scales, w1, w2, lam, e_words, e_scales, unit, tmp, offs, cra, crb, prt, out
):
    nc = tc.nc
    with ExitStack() as ctx:
        keep = ctx.enter_context(tc.tile_pool(name="keep", bufs=1))
        psum = ctx.enter_context(tc.psum_pool(name="psum", bufs=1))

        def load_list(name, src):
            lst = keep.tile(list(src.shape), U16, name=name)
            nc.sync.dma_start(lst[:], src)
            return lst

        def load_words(name, src, width):
            table = keep.tile([P, width], U32, name=name)
            nc.sync.dma_start(table[:].bitcast(I32), src[0].rearrange("p n t -> p (n t)").bitcast(I32))
            return table

        def load_scales(name, src, width, clear, queue):
            table = keep.tile([P, width], U8, name=name)
            clear.memset(table[:].bitcast(I32), 0)
            for q in range(4):
                queue.dma_start(table[32 * q : 32 * q + 4, :].bitcast(I32), src[0, 4 * q : 4 * q + 4, :].bitcast(I32))
            return table

        def load_weight_half(name, w, h):
            raw = keep.tile([P, PACK, H // 2], F32, name=name, align_bytes=64)
            nc.sync.dma_start(raw[:], w.rearrange("(p j) c -> p j c", j=PACK)[:, :, h * (H // 2) : (h + 1) * (H // 2)])
            return raw

        xs_table = load_scales("xs_table", x_scales, T, nc.gpsimd, nc.scalar)
        offs_t = load_list("offs_t", offs)
        xw_table = load_words("xw_table", x_words, T)
        w2_whole = keep.tile([P, PACK, H], F32, name="w2_whole")
        nc.sync.dma_start(w2_whole[:], w2.rearrange("(p j) c -> p j c", j=PACK))
        w2_raw = [w2_whole[:, :, : PACK * 46], w2_whole[:, :, PACK * 46 :]]
        crb_t = load_list("crb_t", crb)
        unit_t = keep.tile([P, PACK], F32, name="unit_t")
        nc.gpsimd.dma_start(unit_t[:], unit.rearrange("(p t) o -> p (t o)", t=PACK))
        w1_raw = [load_weight_half(f"w1_raw{h}", w1, h)[:] for h in range(2)]
        prt_t = load_list("prt_t", prt)
        es_table = load_scales("es_table", e_scales, W, nc.gpsimd, nc.sync)
        ew_table = load_words("ew_table", e_words, W)
        cra_t = load_list("cra_t", cra)
        lam_t = keep.tile([P, PACK, V], F32, name="lam_t")
        nc.sync.dma_start(lam_t[:], lam.rearrange("(p t) v -> p t v", t=PACK))
        tmp_table = keep.tile([P, W], F32, name="tmp_table")
        nc.sync.dma_start(tmp_table[:], tmp)

        gain = keep.tile([P, PACK], F32, name="gain")
        negative = keep.tile([P, PACK], F32, name="negative")
        lam_gain = keep.tile([P, PACK], F32, name="lam_gain")
        slope_gain = keep.tile([P, PACK], F32, name="slope_gain")
        nc.gpsimd.tensor_scalar(gain[:], unit_t[:], 0.6, 0.0, ALU.mult, ALU.add)
        nc.gpsimd.tensor_scalar(negative[:], unit_t[:], 0.0, None, ALU.is_lt)
        nc.gpsimd.tensor_scalar(lam_gain[:], negative[:], -5.0, 2.5, ALU.mult, ALU.add)
        nc.gpsimd.tensor_scalar(slope_gain[:], negative[:], 4.0 / 3.0, -2.0 / 3.0, ALU.mult, ALU.add)

        def gather_packed(name, table, lst, n, dtype, tag):
            picked = keep.tile([P, n], dtype, name=name, tag=tag, align_bytes=64)
            nc.vector.tensor_copy(picked[:], table[:].indirect(lst[:]))
            return picked

        xs = gather_packed("xs", xs_table, offs_t, S, U8, "xs")
        xw = gather_packed("xw", xw_table, offs_t, S, U32, "xw")

        def deal(engine, dst, src):
            dst = dst.rearrange("p t m j -> p m j t")
            src = src.rearrange("p j (m t) -> p m j t", t=PACK)
            if engine is nc.scalar:
                nc.scalar.activation(dst, src, ACT.Copy)
            else:
                nc.vector.tensor_copy(dst, src)

        def weight_tiles(name):
            codes = keep.tile([P, PACK, P], U32, name=f"{name}_codes", align_bytes=64)
            scales = keep.tile([P, PACK, P], U8, name=f"{name}_scales", align_bytes=64)
            return codes, scales

        def project(codes, scales, first_bank):
            banks = []
            for t in range(PACK):
                bank = psum.tile([P, S], F32, name=f"bank{first_bank + t}")
                nc.tensor.matmul_mx(
                    out=bank[:],
                    lhsT=codes[:, t].bitcast(FP8X4),
                    lhsT_scale=scales[:, t],
                    rhs=xw[:].bitcast(FP8X4),
                    rhs_scale=xs[:],
                    start=True,
                    stop=True,
                )
                banks.append(bank)
            return banks

        def evict(name, bank, t):
            row = keep.tile([P, S], F32, name=f"{name}_row{t}")
            nc.scalar.activation(row[:], bank[:], ACT.Copy, scale=gain[:, t : t + 1])
            return row

        w2_codes, w2_scales = weight_tiles("w2")
        w2_dealt = keep.tile([P, PACK, P, PACK], BF16, name="w2_dealt", tag="dealt", align_bytes=64)
        deal(nc.scalar, w2_dealt[:, :, :46], w2_raw[0])
        deal(nc.vector, w2_dealt[:, :, 46:], w2_raw[1])
        for ts in (slice(0, 2), slice(2, 4)):
            nc.vector.quantize_mx(
                out=w2_codes[:, ts].rearrange("p t m -> p (t m)").bitcast(FP8X4),
                scales=w2_scales[:, ts].rearrange("p t m -> p (t m)"),
                in_=w2_dealt[:, ts].rearrange("p t m j -> p (t m j)"),
            )
        yv_banks = project(w2_codes, w2_scales, 0)

        w1_codes, w1_scales = weight_tiles("w1")
        w1_dealt = [
            keep.tile([P, PACK, HALF_M, PACK], BF16, name="w1_dealt0", align_bytes=64),
            keep.tile([P, PACK, HALF_M, PACK], BF16, name="w1_dealt1", tag="dealt", align_bytes=64),
        ]
        deal(nc.scalar, w1_dealt[0][:], w1_raw[0])
        deal(nc.vector, w1_dealt[1][:], w1_raw[1])
        yv_rows = [evict("w2", yv_banks[t], t) for t in range(PACK)]
        for h in range(2):
            for t in range(PACK):
                cols = slice(h * HALF_M, (h + 1) * HALF_M)
                nc.vector.quantize_mx(
                    out=w1_codes[:, t, cols].bitcast(FP8X4),
                    scales=w1_scales[:, t, cols],
                    in_=w1_dealt[h][:, t].rearrange("p m j -> p (m j)"),
                )
        y_banks = project(w1_codes, w1_scales, PACK)
        es = gather_packed("es", es_table, prt_t, Z, U8, "w1_dealt0")
        ew = gather_packed("ew", ew_table, prt_t, Z, U32, "dealt")

        b = keep.tile([P, PACK, V], F32, name="b")
        d = keep.tile([P, PACK, V], F32, name="d")
        slope = keep.tile([P, PACK, V], F32, name="slope")
        pull = keep.tile([P, PACK, V], F32, name="pull")
        share = keep.tile([P, PACK, V], F32, name="share")
        for t in range(PACK):
            nc.gpsimd.tensor_scalar(share[:, t], lam_t[:, t], lam_gain[:, t : t + 1], negative[:, t : t + 1], ALU.mult, ALU.add)
        for t in range(PACK):
            nc.scalar.activation(b[:, t], yv_rows[t][:].indirect(crb_t[:]), ACT.Copy)
            y_row = evict("w1", y_banks[t], t)
            nc.vector.tensor_tensor(d[:, t], y_row[:].indirect(cra_t[:]), b[:, t], ALU.subtract)
        for ts in (slice(0, 2), slice(2, 4)):
            nc.vector.scalar_tensor_tensor(slope[:, ts], d[:, ts], 0.0, share[:, ts], ALU.is_lt, ALU.subtract)
            for t in range(ts.start, ts.stop):
                nc.vector.scalar_tensor_tensor(pull[:, t], slope[:, t], slope_gain[:, t : t + 1], d[:, t], ALU.mult, ALU.mult)

        temp = keep.tile([P, Z], F32, name="temp", tag="w1_row3")
        nc.scalar.activation(temp[:], tmp_table[:].indirect(prt_t[:]), ACT.Copy)

        banks = []
        for h in range(V // P):
            vs = slice(h * P, (h + 1) * P)
            hid = keep.tile([P, P, PACK], BF16, name=f"hid{h}", align_bytes=64)
            nc.vector.tensor_tensor(
                hid[:].rearrange("p (c i) t -> p c t i", i=4),
                pull[:, :, vs].rearrange("p t (c i) -> p c t i", i=4),
                b[:, :, vs].rearrange("p t (c i) -> p c t i", i=4),
                ALU.add,
            )
            hid_codes = keep.tile([P, P], U32, name=f"hid_codes{h}", align_bytes=64)
            hid_scales = keep.tile([P, P], U8, name=f"hid_scales{h}", align_bytes=64)
            nc.vector.quantize_mx(
                out=hid_codes[:].bitcast(FP8X4), scales=hid_scales[:], in_=hid[:].rearrange("p v t -> p (v t)")
            )
            bank = psum.tile([P, Z], F32, name=f"bank{h}")
            nc.tensor.matmul_mx(
                out=bank[:],
                lhsT=hid_codes[:].bitcast(FP8X4),
                lhsT_scale=hid_scales[:],
                rhs=ew[:].bitcast(FP8X4),
                rhs_scale=es[:],
                start=True,
                stop=True,
            )
            banks.append(bank)
        for h in range(V // P):
            lt = keep.tile([P, Z], F32, name=f"lt{h}")
            neg_mean = keep.tile([P, 1], F32, name=f"neg_mean{h}")
            nc.vector.scalar_tensor_tensor(lt[:], banks[h][:], -1.0 / Z, temp[:], ALU.mult, ALU.mult, accum_out=neg_mean[:])
            gate = keep.tile([P, Z], F32, name=f"gate{h}")
            nc.scalar.activation(gate[:], lt[:], ACT.Sigmoid, scale=-float(Z), bias=neg_mean[:])
            result = keep.tile([P, Z], F32, name=f"result{h}")
            nc.vector.scalar_tensor_tensor(result[:], lt[:], -float(Z), gate[:], ALU.mult, ALU.mult)
            nc.sync.dma_start(out[h * P : (h + 1) * P, :], result[:])
